import numpy as np
import ml_dtypes


def mxq(x, axis, fmt="e4m3"):
    dtype, down = {"e4m3": (ml_dtypes.float8_e4m3fn, 7), "e5m2": (ml_dtypes.float8_e5m2, 14)}[fmt]
    v = np.moveaxis(np.asarray(x, np.float32).astype(ml_dtypes.bfloat16).astype(np.float64), axis, -1)
    blocks = v.reshape(v.shape[:-1] + (-1, 32))
    amax = np.abs(blocks).max(-1, keepdims=True)
    byte = np.maximum(np.where(amax > 0, np.frexp(amax)[1] - 1 + 127, 0) - down, 1)
    scale = np.exp2(byte - 127.0)
    codes = (blocks / scale).astype(np.float32).astype(dtype).astype(np.float64)
    return np.moveaxis((codes * scale).reshape(v.shape), -1, axis)


WIDE = False


def mx_kscale(k):
    if not WIDE:
        return np.ones(k)
    levels = np.array([10, -10, 5, -5, 0])
    if k % 512:
        return np.exp2(np.random.permutation(np.resize(levels, k // 32))).repeat(32)
    a = np.empty((k // 512, 16))
    for p in range(k // 512):
        a[p, :8] = np.random.permutation(np.resize(levels, 8))
        for g in range(8):
            far = levels[np.abs(levels - a[p, g]) >= 10]
            a[p, g + 8] = far[np.random.randint(len(far))]
    return np.exp2(a.ravel()).repeat(32)


def f64(x):
    return np.asarray(x).astype(np.float64)


def striped(idx):
    return np.tile(idx.reshape(-1, 16).T, (8, 1)).astype(np.uint16)


def unstriped(offs):
    return offs[:16].T.reshape(-1).astype(np.int64)


def pack_weight(w):
    k, n = w.shape
    w = f64(np.asarray(w, np.float32).astype(ml_dtypes.bfloat16)).reshape(k // 32, 32, n)
    amax = np.abs(w).max(1)
    byte = np.clip(np.where(amax > 0, np.frexp(amax)[1] - 1 + 127 - 7, 1), 1, 254)
    scaled = (w * np.exp2(127.0 - byte)[:, None, :]).reshape(k, n).astype(np.float32)
    words = np.ascontiguousarray(scaled.reshape(k // 512, 128, 4, n).transpose(0, 1, 3, 2)).astype(ml_dtypes.float8_e4m3fn).view(np.uint8)
    return words, np.ascontiguousarray(byte.astype(np.uint8).reshape(k // 512, 16, n))


def unpack_weight(words, scales):
    g, p, n, _ = words.shape
    vals = np.ascontiguousarray(words).view(ml_dtypes.float8_e4m3fn).astype(np.float64) * np.repeat(np.exp2(scales.astype(np.float64) - 127.0), 8, axis=1)[..., None]
    return vals.transpose(0, 1, 3, 2).reshape(g * 512, n)


K, T, E, C, N = 512, 4096, 8, 128, 128


def by_expert(wq, xq):
    return np.concatenate([wq[e].T @ xq[:, e * C:(e + 1) * C] for e in range(E)], axis=1)


def setup_inputs():
    n = np.random.standard_normal
    s = mx_kscale(K)[:, None]
    packed = [pack_weight(m) for m in n((E, K, N)) / np.sqrt(K) / s[None]]
    return {
        "xT": (n((K, T)) * s).astype(np.float32),
        "w_words": np.stack([m[0] for m in packed]),
        "w_scales": np.stack([m[1] for m in packed]),
        "gate": np.tile(np.random.uniform(0.2, 1.0, E * C), (N, 1)).astype(np.float32),
        "offs": striped(np.random.permutation(T)[:E * C]),
    }


def reference(xT, w_words, w_scales, gate, offs):
    idx = unstriped(offs)
    xq = mxq(f64(xT)[:, idx], 0, "e4m3")
    w = np.stack([unpack_weight(w_words[e], w_scales[e]) for e in range(E)])
    y = by_expert(w, xq)
    out = np.zeros((N, T))
    out[:, idx] = f64(gate) * y
    return out

@@ -1,0 +1,110 @@
+from contextlib import ExitStack
+
+import concourse.mybir as mybir
+
+K, T, E, C, N = 512, 4096, 8, 128, 128
+SLOTS = E * C
+FLOPS = 2 * K * N * SLOTS
+
+F32 = mybir.dt.float32
+BF16 = mybir.dt.bfloat16
+U32 = mybir.dt.uint32
+I32 = mybir.dt.int32
+U16 = mybir.dt.uint16
+U8 = mybir.dt.uint8
+FP8X4 = mybir.dt.float8_e4m3fn_x4
+
+P = 128
+PACK = 4
+PIECE = 512
+PIECES = SLOTS // PIECE
+OFFS_COLS = PIECE // 16
+
+
+def tile_routed_moe_kernel(tc, xT, w_words, w_scales, gate, offs, out):
+    nc = tc.nc
+    with ExitStack() as ctx:
+        held = ctx.enter_context(tc.tile_pool(name="held", bufs=1))
+        psum = ctx.enter_context(tc.psum_pool(name="psum", bufs=1))
+
+        offs_t = held.tile([P, SLOTS // 16], U16, name="offs_t")
+        nc.sync.dma_start(offs_t[:], offs)
+
+        rows = xT.rearrange("(p t) n -> t p n", t=PACK)
+        planes = []
+        for t in range(PACK):
+            plane = held.tile([P, T], F32, name="plane%d" % t)
+            nc.sync.dma_start(plane[:], rows[t])
+            planes.append(plane)
+
+        w_sc = held.tile([P, E, N], U8, name="w_sc", align_bytes=64)
+        nc.vector.memset(w_sc[:].rearrange("p e n -> p (e n)").bitcast(I32), 0)
+        sc_rows = w_scales.rearrange("e a q n -> q (e a) n")
+        for q in range(4):
+            nc.sync.dma_start(w_sc[32 * q : 32 * q + 4].bitcast(I32), sc_rows[4 * q : 4 * q + 4].bitcast(I32))
+
+        w_codes = held.tile([P, E, N], I32, name="w_codes", align_bytes=64)
+        nc.sync.dma_start(w_codes[:], w_words.rearrange("e a p n r -> p (e a) (n r)").bitcast(I32))
+
+        gate_t = held.tile([P, SLOTS], F32, name="gate_t")
+        nc.sync.dma_start(gate_t[:], gate)
+
+        win = held.tile([P, T], F32, name="win")
+        nc.vector.memset(win[:], 0.0)
+
+        warm_in = held.tile([P, 8], F32, name="warm_in")
+        warm_out = held.tile([P, 8], F32, name="warm_out")
+        nc.gpsimd.memset(warm_in[:], 0.0)
+        nc.scalar.copy(warm_out[:], warm_in[:])
+
+        grouped = [held.tile([P, PIECE, PACK], BF16, name="grouped%d" % h, align_bytes=64) for h in range(PIECES)]
+
+        def gather(t, h):
+            nc.vector.tensor_copy(
+                grouped[h][:, :, t], planes[t][:].indirect(offs_t[:, h * OFFS_COLS : (h + 1) * OFFS_COLS])
+            )
+
+        for t in range(PACK - 1):
+            for h in range(PIECES):
+                gather(t, h)
+
+        for h in range(PIECES):
+            gather(PACK - 1, h)
+
+        cuts = [(0, 256), (256, 128), (384, 128), (512, 512)]
+        sums = [held.tile([P, PIECE], F32, name="y%d" % h) for h in range(PIECES)]
+        for i, (s0, n) in enumerate(cuts):
+            h = s0 // PIECE
+            r0 = s0 - h * PIECE
+            x_codes = held.tile([P, n], U32, name="x_codes%d" % i, align_bytes=64)
+            x_sc = held.tile([P, n], U8, name="x_sc%d" % i, align_bytes=64)
+            nc.vector.quantize_mx(
+                out=x_codes[:].bitcast(FP8X4),
+                scales=x_sc[:],
+                in_=grouped[h][:, r0 : r0 + n, :].rearrange("p n t -> p (n t)"),
+            )
+            acc = psum.tile([P, n], F32, name="acc%d" % i)
+            for j in range(n // C):
+                e = s0 // C + j
+                cols = slice(j * C, (j + 1) * C)
+                nc.tensor.matmul_mx(
+                    out=acc[:, cols],
+                    lhsT=w_codes[:, e, :].bitcast(FP8X4),
+                    lhsT_scale=w_sc[:, e, :],
+                    rhs=x_codes[:, cols].bitcast(FP8X4),
+                    rhs_scale=x_sc[:, cols],
+                    start=True,
+                    stop=True,
+                )
+            nc.scalar.copy(sums[h][:, r0 : r0 + n], acc[:])
+
+        for h in range(PIECES):
+            nc.vector.tensor_tensor(
+                win[:].indirect(offs_t[:, h * OFFS_COLS : (h + 1) * OFFS_COLS]),
+                sums[h][:],
+                gate_t[:, h * PIECE : (h + 1) * PIECE],
+                mybir.AluOpType.mult,
+            )
+
+        nc.sync.dma_start(out[:, 0 : T // 2], win[:, 0 : T // 2])
+        nc.scalar.dma_start(out[:, T // 2 : T], win[:, T // 2 : T])

@@ -64,12 +64,19 @@ def tile_routed_moe_kernel(tc, xT, w_words, w_scales, gate, offs, out):
                 grouped[h][:, :, t], planes[t][:].indirect(offs_t[:, h * OFFS_COLS : (h + 1) * OFFS_COLS])
             )
 
-        for t in range(PACK - 1):
+        loose = [held.tile([P, PIECE], F32, name="loose%d" % t) for t in (2, 3)]
+
+        def gather_loose(t):
+            nc.vector.tensor_copy(loose[t - 2][:], planes[t][:].indirect(offs_t[:, OFFS_COLS : 2 * OFFS_COLS]))
+            nc.scalar.copy(grouped[1][:, :, t], loose[t - 2][:])
+
+        for t in range(2):
             for h in range(PIECES):
                 gather(t, h)
-
-        for h in range(PIECES):
-            gather(PACK - 1, h)
+        gather_loose(2)
+        gather(2, 0)
+        gather_loose(3)
+        gather(3, 0)
 
         cuts = [(0, 256), (256, 128), (384, 128), (512, 512)]
         sums = [held.tile([P, PIECE], F32, name="y%d" % h) for h in range(PIECES)]

@@ -64,21 +64,22 @@ def tile_routed_moe_kernel(tc, xT, w_words, w_scales, gate, offs, out):
                 grouped[h][:, :, t], planes[t][:].indirect(offs_t[:, h * OFFS_COLS : (h + 1) * OFFS_COLS])
             )
 
+        cuts = [(0, 256), (256, 128), (384, 128), (512, 512)]
+
         loose = [held.tile([P, PIECE], F32, name="loose%d" % t) for t in (2, 3)]
 
         def gather_loose(t):
-            nc.vector.tensor_copy(loose[t - 2][:], planes[t][:].indirect(offs_t[:, OFFS_COLS : 2 * OFFS_COLS]))
-            nc.scalar.copy(grouped[1][:, :, t], loose[t - 2][:])
+            nc.vector.tensor_copy(loose[t - 2][:], planes[t][:].indirect(offs_t[:, 0:OFFS_COLS]))
+            for s0, n in cuts[:3]:
+                nc.scalar.copy(grouped[0][:, s0 : s0 + n, t], loose[t - 2][:, s0 : s0 + n])
 
         for t in range(2):
             for h in range(PIECES):
                 gather(t, h)
         gather_loose(2)
-        gather(2, 0)
+        gather(2, 1)
         gather_loose(3)
-        gather(3, 0)
-
-        cuts = [(0, 256), (256, 128), (384, 128), (512, 512)]
+        gather(3, 1)
         sums = [held.tile([P, PIECE], F32, name="y%d" % h) for h in range(PIECES)]
         for i, (s0, n) in enumerate(cuts):
             h = s0 // PIECE

@@ -81,11 +81,15 @@ def tile_routed_moe_kernel(tc, xT, w_words, w_scales, gate, offs, out):
         gather_loose(3)
         gather(3, 1)
         sums = [held.tile([P, PIECE], F32, name="y%d" % h) for h in range(PIECES)]
+        codes_before = None
         for i, (s0, n) in enumerate(cuts):
             h = s0 // PIECE
             r0 = s0 - h * PIECE
             x_codes = held.tile([P, n], U32, name="x_codes%d" % i, align_bytes=64)
             x_sc = held.tile([P, n], U8, name="x_sc%d" % i, align_bytes=64)
+            if s0 == PIECE:
+                nc.vector.tensor_copy(x_codes[:, 0:16].bitcast(I32), codes_before[:, 0:16].bitcast(I32))
+            codes_before = x_codes
             nc.vector.quantize_mx(
                 out=x_codes[:].bitcast(FP8X4),
                 scales=x_sc[:],

@@ -28,7 +28,6 @@ def tile_routed_moe_kernel(tc, xT, w_words, w_scales, gate, offs, out):
         psum = ctx.enter_context(tc.psum_pool(name="psum", bufs=1))
 
         offs_t = held.tile([P, SLOTS // 16], U16, name="offs_t")
-        nc.sync.dma_start(offs_t[:], offs)
 
         rows = xT.rearrange("(p t) n -> t p n", t=PACK)
         planes = []
@@ -36,6 +35,8 @@ def tile_routed_moe_kernel(tc, xT, w_words, w_scales, gate, offs, out):
             plane = held.tile([P, T], F32, name="plane%d" % t)
             nc.sync.dma_start(plane[:], rows[t])
             planes.append(plane)
+            if t == 0:
+                nc.sync.dma_start(offs_t[:], offs)
 
         w_sc = held.tile([P, E, N], U8, name="w_sc", align_bytes=64)
         nc.vector.memset(w_sc[:].rearrange("p e n -> p (e n)").bitcast(I32), 0)

@@ -65,13 +65,13 @@ def tile_routed_moe_kernel(tc, xT, w_words, w_scales, gate, offs, out):
                 grouped[h][:, :, t], planes[t][:].indirect(offs_t[:, h * OFFS_COLS : (h + 1) * OFFS_COLS])
             )
 
-        cuts = [(0, 256), (256, 128), (384, 128), (512, 512)]
+        cuts = [(0, 256), (256, 128), (384, 64), (448, 64), (512, 512)]
 
         loose = [held.tile([P, PIECE], F32, name="loose%d" % t) for t in (2, 3)]
 
         def gather_loose(t):
             nc.vector.tensor_copy(loose[t - 2][:], planes[t][:].indirect(offs_t[:, 0:OFFS_COLS]))
-            for s0, n in cuts[:3]:
+            for s0, n in cuts[:4]:
                 nc.scalar.copy(grouped[0][:, s0 : s0 + n, t], loose[t - 2][:, s0 : s0 + n])
 
         for t in range(2):
@@ -97,9 +97,9 @@ def tile_routed_moe_kernel(tc, xT, w_words, w_scales, gate, offs, out):
                 in_=grouped[h][:, r0 : r0 + n, :].rearrange("p n t -> p (n t)"),
             )
             acc = psum.tile([P, n], F32, name="acc%d" % i)
-            for j in range(n // C):
+            for j in range(max(1, n // C)):
                 e = s0 // C + j
-                cols = slice(j * C, (j + 1) * C)
+                cols = slice(j * C, j * C + min(n, C))
                 nc.tensor.matmul_mx(
                     out=acc[:, cols],
                     lhsT=w_codes[:, e, :].bitcast(FP8X4),

@@ -82,20 +82,18 @@ def tile_routed_moe_kernel(tc, xT, w_words, w_scales, gate, offs, out):
         gather_loose(3)
         gather(3, 1)
         sums = [held.tile([P, PIECE], F32, name="y%d" % h) for h in range(PIECES)]
-        codes_before = None
+        read_before = None
         for i, (s0, n) in enumerate(cuts):
             h = s0 // PIECE
             r0 = s0 - h * PIECE
             x_codes = held.tile([P, n], U32, name="x_codes%d" % i, align_bytes=64)
             x_sc = held.tile([P, n], U8, name="x_sc%d" % i, align_bytes=64)
+            values = grouped[h][:, r0 : r0 + n, :].rearrange("p n t -> p (n t)")
             if s0 == PIECE:
-                nc.vector.tensor_copy(x_codes[:, 0:16].bitcast(I32), codes_before[:, 0:16].bitcast(I32))
-            codes_before = x_codes
-            nc.vector.quantize_mx(
-                out=x_codes[:].bitcast(FP8X4),
-                scales=x_sc[:],
-                in_=grouped[h][:, r0 : r0 + n, :].rearrange("p n t -> p (n t)"),
-            )
+                nc.vector.memset(x_codes[:, 0:16].bitcast(I32), 0)
+                nc.vector.tensor_copy(read_before[:, 0:32].bitcast(I32), x_codes[:, 0:16].bitcast(I32))
+            read_before = values
+            nc.vector.quantize_mx(out=x_codes[:].bitcast(FP8X4), scales=x_sc[:], in_=values)
             acc = psum.tile([P, n], F32, name="acc%d" % i)
             for j in range(max(1, n // C)):
                 e = s0 // C + j

from contextlib import ExitStack

import concourse.mybir as mybir

K, T, E, C, N = 512, 4096, 8, 128, 128
SLOTS = E * C
FLOPS = 2 * K * N * SLOTS

F32 = mybir.dt.float32
BF16 = mybir.dt.bfloat16
U32 = mybir.dt.uint32
I32 = mybir.dt.int32
U16 = mybir.dt.uint16
U8 = mybir.dt.uint8
FP8X4 = mybir.dt.float8_e4m3fn_x4

P = 128
PACK = 4
PIECE = 512
PIECES = SLOTS // PIECE
OFFS_COLS = PIECE // 16


def tile_routed_moe_kernel(tc, xT, w_words, w_scales, gate, offs, out):
    nc = tc.nc
    with ExitStack() as ctx:
        held = ctx.enter_context(tc.tile_pool(name="held", bufs=1))
        psum = ctx.enter_context(tc.psum_pool(name="psum", bufs=1))

        offs_t = held.tile([P, SLOTS // 16], U16, name="offs_t")

        rows = xT.rearrange("(p t) n -> t p n", t=PACK)
        planes = []
        for t in range(PACK):
            plane = held.tile([P, T], F32, name="plane%d" % t)
            nc.sync.dma_start(plane[:], rows[t])
            planes.append(plane)
            if t == 0:
                nc.sync.dma_start(offs_t[:], offs)

        w_sc = held.tile([P, E, N], U8, name="w_sc", align_bytes=64)
        nc.vector.memset(w_sc[:].rearrange("p e n -> p (e n)").bitcast(I32), 0)
        sc_rows = w_scales.rearrange("e a q n -> q (e a) n")
        for q in range(4):
            nc.sync.dma_start(w_sc[32 * q : 32 * q + 4].bitcast(I32), sc_rows[4 * q : 4 * q + 4].bitcast(I32))

        w_codes = held.tile([P, E, N], I32, name="w_codes", align_bytes=64)
        nc.sync.dma_start(w_codes[:], w_words.rearrange("e a p n r -> p (e a) (n r)").bitcast(I32))

        gate_t = held.tile([P, SLOTS], F32, name="gate_t")
        nc.sync.dma_start(gate_t[:], gate)

        win = held.tile([P, T], F32, name="win")
        nc.vector.memset(win[:], 0.0)

        warm_in = held.tile([P, 8], F32, name="warm_in")
        warm_out = held.tile([P, 8], F32, name="warm_out")
        nc.gpsimd.memset(warm_in[:], 0.0)
        nc.scalar.copy(warm_out[:], warm_in[:])

        grouped = [held.tile([P, PIECE, PACK], BF16, name="grouped%d" % h, align_bytes=64) for h in range(PIECES)]

        def gather(t, h):
            nc.vector.tensor_copy(
                grouped[h][:, :, t], planes[t][:].indirect(offs_t[:, h * OFFS_COLS : (h + 1) * OFFS_COLS])
            )

        cuts = [(0, 256), (256, 128), (384, 64), (448, 64), (512, 512)]

        loose = [held.tile([P, PIECE], F32, name="loose%d" % t) for t in (2, 3)]

        def gather_loose(t):
            nc.vector.tensor_copy(loose[t - 2][:], planes[t][:].indirect(offs_t[:, 0:OFFS_COLS]))
            for s0, n in cuts[:4]:
                nc.scalar.copy(grouped[0][:, s0 : s0 + n, t], loose[t - 2][:, s0 : s0 + n])

        for t in range(2):
            for h in range(PIECES):
                gather(t, h)
        gather_loose(2)
        gather(2, 1)
        gather_loose(3)
        gather(3, 1)
        sums = [held.tile([P, PIECE], F32, name="y%d" % h) for h in range(PIECES)]
        read_before = None
        for i, (s0, n) in enumerate(cuts):
            h = s0 // PIECE
            r0 = s0 - h * PIECE
            x_codes = held.tile([P, n], U32, name="x_codes%d" % i, align_bytes=64)
            x_sc = held.tile([P, n], U8, name="x_sc%d" % i, align_bytes=64)
            values = grouped[h][:, r0 : r0 + n, :].rearrange("p n t -> p (n t)")
            if s0 == PIECE:
                nc.vector.memset(x_codes[:, 0:16].bitcast(I32), 0)
                nc.vector.tensor_copy(read_before[:, 0:32].bitcast(I32), x_codes[:, 0:16].bitcast(I32))
            read_before = values
            nc.vector.quantize_mx(out=x_codes[:].bitcast(FP8X4), scales=x_sc[:], in_=values)
            acc = psum.tile([P, n], F32, name="acc%d" % i)
            for j in range(max(1, n // C)):
                e = s0 // C + j
                cols = slice(j * C, j * C + min(n, C))
                nc.tensor.matmul_mx(
                    out=acc[:, cols],
                    lhsT=w_codes[:, e, :].bitcast(FP8X4),
                    lhsT_scale=w_sc[:, e, :],
                    rhs=x_codes[:, cols].bitcast(FP8X4),
                    rhs_scale=x_sc[:, cols],
                    start=True,
                    stop=True,
                )
            nc.scalar.copy(sums[h][:, r0 : r0 + n], acc[:])

        for h in range(PIECES):
            nc.vector.tensor_tensor(
                win[:].indirect(offs_t[:, h * OFFS_COLS : (h + 1) * OFFS_COLS]),
                sums[h][:],
                gate_t[:, h * PIECE : (h + 1) * PIECE],
                mybir.AluOpType.mult,
            )

        nc.sync.dma_start(out[:, 0 : T // 2], win[:, 0 : T // 2])
        nc.scalar.dma_start(out[:, T // 2 : T], win[:, T // 2 : T])
